import numpy as np
import ml_dtypes


def mxq(x, axis, fmt="e4m3"):
    dtype, down = {"e4m3": (ml_dtypes.float8_e4m3fn, 7), "e5m2": (ml_dtypes.float8_e5m2, 14)}[fmt]
    v = np.moveaxis(np.asarray(x, np.float32).astype(ml_dtypes.bfloat16).astype(np.float64), axis, -1)
    blocks = v.reshape(v.shape[:-1] + (-1, 32))
    amax = np.abs(blocks).max(-1, keepdims=True)
    byte = np.maximum(np.where(amax > 0, np.frexp(amax)[1] - 1 + 127, 0) - down, 1)
    scale = np.exp2(byte - 127.0)
    codes = (blocks / scale).astype(np.float32).astype(dtype).astype(np.float64)
    return np.moveaxis((codes * scale).reshape(v.shape), -1, axis)


WIDE = False


def mx_kscale(k):
    if not WIDE:
        return np.ones(k)
    levels = np.array([10, -10, 5, -5, 0])
    if k % 512:
        return np.exp2(np.random.permutation(np.resize(levels, k // 32))).repeat(32)
    a = np.empty((k // 512, 16))
    for p in range(k // 512):
        a[p, :8] = np.random.permutation(np.resize(levels, 8))
        for g in range(8):
            far = levels[np.abs(levels - a[p, g]) >= 10]
            a[p, g + 8] = far[np.random.randint(len(far))]
    return np.exp2(a.ravel()).repeat(32)


def f64(x):
    return np.asarray(x).astype(np.float64)


def striped(idx):
    return np.tile(idx.reshape(-1, 16).T, (8, 1)).astype(np.uint16)


def unstriped(offs):
    return offs[:16].T.reshape(-1).astype(np.int64)


def striped8(idx):
    return np.concatenate([x.reshape(-1, 16).T for x in idx]).astype(np.uint16)


def runs(offs, k):
    lists = np.stack([offs[16 * r : 16 * r + 16].T.reshape(-1) for r in range(8)]).astype(np.int64)
    return lists[np.arange(k) % 512 // 64]


def pack_weight(w):
    k, n = w.shape
    w = f64(np.asarray(w, np.float32).astype(ml_dtypes.bfloat16)).reshape(k // 32, 32, n)
    amax = np.abs(w).max(1)
    byte = np.clip(np.where(amax > 0, np.frexp(amax)[1] - 1 + 127 - 7, 1), 1, 254)
    scaled = (w * np.exp2(127.0 - byte)[:, None, :]).reshape(k, n).astype(np.float32)
    words = np.ascontiguousarray(scaled.reshape(k // 512, 128, 4, n).transpose(0, 1, 3, 2)).astype(ml_dtypes.float8_e4m3fn).view(np.uint8)
    return words, np.ascontiguousarray(byte.astype(np.uint8).reshape(k // 512, 16, n))


def unpack_weight(words, scales):
    g, p, n, _ = words.shape
    vals = np.ascontiguousarray(words).view(ml_dtypes.float8_e4m3fn).astype(np.float64) * np.repeat(np.exp2(scales.astype(np.float64) - 127.0), 8, axis=1)[..., None]
    return vals.transpose(0, 1, 3, 2).reshape(g * 512, n)


K, T, S, N, H = 512, 2048, 512, 512, 512


def setup_inputs():
    n = np.random.standard_normal
    s = mx_kscale(K)[:, None]
    u = mx_kscale(H)
    packed_xT = pack_weight(n((K, T)) * s)
    return {
        "x_words": packed_xT[0],
        "x_scales": packed_xT[1],
        "w1": (n((K, H)) / np.sqrt(K) / s).astype(np.float32),
        "gn": (np.random.uniform(0.5, 1.5, (H, 1)) * u[:, None]).astype(np.float32),
        "w2": (n((H, N)) / np.sqrt(H) / u[:, None]).astype(np.float32),
        "offs": striped(np.random.permutation(T)[:S]),
        "n1": striped8(np.stack([np.random.permutation(S) for _ in range(8)])),
        "n2": striped8(np.stack([np.random.permutation(S) for _ in range(8)])),
        "n3": striped8(np.stack([np.random.permutation(S) for _ in range(8)])),
        "n4": striped8(np.stack([np.random.permutation(S) for _ in range(8)])),
    }


def reference(x_words, x_scales, w1, gn, w2, offs, n1, n2, n3, n4):
    xq = unpack_weight(x_words, x_scales)[:, unstriped(offs)]
    y = mxq(f64(w1), 0, "e4m3").T @ xq
    z = f64(gn) * (y * (y[np.arange(H)[:, None], runs(n1, H)] - (y[np.arange(H)[:, None], runs(n2, H)])))
    h = mxq(f64(w2), 0, "e4m3").T @ mxq(z, 0, "e4m3")
    return (h - (h[np.arange(N)[:, None], runs(n3, N)])) / (np.abs(y) + np.abs(y[np.arange(H)[:, None], runs(n4, H)]) + 0.5)

@@ -1,0 +1,222 @@
+from contextlib import ExitStack
+
+import concourse.mybir as mybir
+
+K, T, S, N, H = 512, 2048, 512, 512, 512
+FLOPS = 2 * K * H * S + 2 * H * N * S
+
+F32 = mybir.dt.float32
+BF16 = mybir.dt.bfloat16
+I32 = mybir.dt.int32
+U32 = mybir.dt.uint32
+U16 = mybir.dt.uint16
+U8 = mybir.dt.uint8
+FP8X4 = mybir.dt.float8_e4m3fn_x4
+ALU = mybir.AluOpType
+ACT = mybir.ActivationFunctionType
+
+P = 128
+PACK = 4
+WIN = 2 * S
+HALF = S // 2
+
+
+def tile_picked_skipnormbwind_none_p_kernel(
+    tc, x_words, x_scales, w1, gn, w2, offs, n1, n2, n3, n4, out
+):
+    nc = tc.nc
+    with ExitStack() as ctx:
+        keep = ctx.enter_context(tc.tile_pool(name="keep", bufs=1))
+        psum = ctx.enter_context(tc.psum_pool(name="psum", bufs=1))
+
+        def sb(name, shape, dtype, tag=None):
+            return keep.tile(shape, dtype, name=name, tag=tag or name, align_bytes=64)
+
+        lists = {}
+        for name in ("offs", "n1", "n2", "n3", "n4"):
+            lists[name] = sb("list_" + name, [P, S // 16], U16)
+
+        def entries(name, lo, hi):
+            return lists[name][:, lo // 16 : hi // 16]
+
+        xs = sb("xs", [P, T], U8)
+        nc.vector.memset(xs[:].bitcast(I32), 0)
+        nc.sync.dma_start(lists["offs"][:], offs)
+        nc.sync.dma_start(lists["n2"][:], n2)
+        nc.sync.dma_start(lists["n1"][:], n1)
+        nc.sync.dma_start(lists["n4"][:], n4)
+        xw = sb("xw", [P, T], I32, tag="big_load")
+        nc.sync.dma_start(xw[:], x_words[0].rearrange("p n t -> p (n t)").bitcast(I32))
+        half = H // 2
+        w1_raw = [sb("w1_raw%d" % u, [P, PACK, half], F32) for u in range(2)]
+        w1_rows = w1.rearrange("(p j) c -> p j c", j=PACK)
+        for u in range(2):
+            nc.sync.dma_start(w1_raw[u][:], w1_rows[:, :, u * half : (u + 1) * half])
+        nc.sync.dma_start(lists["n3"][:], n3)
+
+        warm = sb("warm", [P, 8], F32)
+        warm2 = sb("warm2", [P, 8], F32)
+        nc.vector.memset(warm[:], 1.0)
+        nc.scalar.activation(warm2[:], warm[:], ACT.Abs_reciprocal_sqrt)
+        for q in range(4):
+            nc.scalar.dma_start(
+                xs[32 * q : 32 * q + 4, :].bitcast(I32),
+                x_scales[0, 4 * q : 4 * q + 4, :].bitcast(I32),
+            )
+        gain = sb("gain", [P, PACK], F32)
+        nc.gpsimd.dma_start(gain[:], gn.rearrange("(p t) o -> p (t o)", t=PACK))
+
+        win = [sb("win%d" % t, [P, WIN], F32) for t in range(PACK)]
+        awin = [sb("awin%d" % t, [P, WIN], F32) for t in range(PACK)]
+        for t in range(PACK):
+            nc.vector.memset(win[t][:, S:], 0.0)
+        for t in range(PACK):
+            nc.gpsimd.memset(awin[t][:, S:], 0.0)
+
+        xg_s = sb("xg_s", [P, S], U8)
+        xg_w = sb("xg_w", [P, S], I32)
+        nc.vector.tensor_copy(xg_w[:].bitcast(U32), xw[:].bitcast(U32).indirect(lists["offs"][:]))
+        nc.vector.tensor_copy(xg_s[:], xs[:].indirect(lists["offs"][:]))
+
+        w2_raw = sb("w2_raw", [P, PACK, N], F32, tag="big_load")
+        nc.sync.dma_start(w2_raw[:], w2.rearrange("(p j) c -> p j c", j=PACK))
+
+        def deal(engine_copy, grouped, raw, m0, m1, raw_m0):
+            engine_copy(
+                grouped[:, :, m0:m1, :].rearrange("p t m j -> p m j t"),
+                raw[:].rearrange("p j (m t) -> p m j t", t=PACK)[:, m0 - raw_m0 : m1 - raw_m0],
+            )
+
+        w1_b = sb("w1_b", [P, PACK, P, PACK], BF16)
+        deal(nc.scalar.copy, w1_b, w1_raw[0], 0, 64, 0)
+        deal(nc.vector.tensor_copy, w1_b, w1_raw[1], 64, 112, 64)
+        deal(nc.scalar.copy, w1_b, w1_raw[1], 112, 128, 64)
+        w1_c = sb("w1_c", [P, PACK, P], U32)
+        w1_s = sb("w1_s", [P, PACK, P], U8)
+        y_ps = [psum.tile([P, S], F32, name="y_ps%d" % t) for t in range(PACK)]
+        for t in range(PACK):
+            nc.vector.quantize_mx(
+                out=w1_c[:, t, :].bitcast(FP8X4),
+                scales=w1_s[:, t, :],
+                in_=w1_b[:, t].rearrange("p m j -> p (m j)"),
+            )
+            nc.tensor.matmul_mx(
+                out=y_ps[t][:],
+                lhsT=w1_c[:, t, :].bitcast(FP8X4),
+                lhsT_scale=w1_s[:, t, :],
+                rhs=xg_w[:].bitcast(FP8X4),
+                rhs_scale=xg_s[:],
+                start=True,
+                stop=True,
+            )
+
+        for t in range(PACK):
+            nc.scalar.activation(win[t][:, :S], y_ps[t][:], ACT.Copy, scale=gain[:, t : t + 1])
+
+        acopy = [sb("acopy%d" % t, [P, S], F32) for t in range(PACK)]
+
+        def size_of_y(t):
+            nc.scalar.activation(awin[t][:, :S], y_ps[t][:], ACT.Abs)
+            nc.sync.dma_start(acopy[t][:], awin[t][:, :S])
+
+        size_of_y(0)
+        size_of_y(1)
+        w2_b = sb("w2_b", [P, PACK, P, PACK], BF16)
+        deal(nc.scalar.copy, w2_b, w2_raw, 0, 128, 0)
+        size_of_y(2)
+        size_of_y(3)
+
+        z_planes = sb("z_planes", [P, PACK, S], BF16)
+
+        def z_plane(t, lo, hi, name, tag=None):
+            g2 = sb("g2_" + name, [P, hi - lo], F32, tag=tag)
+            d = sb("d_" + name, [P, hi - lo], F32)
+            nc.vector.tensor_copy(g2[:], win[t][:].indirect(entries("n2", lo, hi)))
+            nc.vector.tensor_tensor(d[:], win[t][:].indirect(entries("n1", lo, hi)), g2[:], ALU.subtract)
+            nc.vector.tensor_tensor(z_planes[:, t, lo:hi], d[:], y_ps[t][:, lo:hi], ALU.mult)
+
+        den = {}
+
+        def denominator(t, tag):
+            den[t] = sb("den%d" % t, [P, S], F32, tag=tag)
+            nc.vector.tensor_tensor(den[t][:], awin[t][:].indirect(lists["n4"][:]), acopy[t][:], ALU.add)
+
+        recip = {}
+
+        def reciprocal(t):
+            root = sb("root%d" % t, [P, S], F32)
+            recip[t] = sb("recip%d" % t, [P, S], F32)
+            nc.scalar.activation(root[:], den[t][:], ACT.Abs_reciprocal_sqrt, bias=0.5)
+            nc.scalar.activation(recip[t][:], root[:], ACT.Square)
+
+        z_plane(0, 0, S, "0")
+        z_plane(1, 0, S, "1")
+        w2_c = sb("w2_c", [P, N], U32)
+        w2_s = sb("w2_s", [P, N], U8)
+        denominator(0, "d_1")
+        reciprocal(0)
+        denominator(1, "acopy0")
+        reciprocal(1)
+        nc.vector.quantize_mx(
+            out=w2_c[:].bitcast(FP8X4), scales=w2_s[:], in_=w2_b[:].rearrange("p t m j -> p (t m j)")
+        )
+        z_plane(2, 0, S, "2", tag="acopy1")
+        z_plane(3, 0, HALF, "3a")
+        z_plane(3, HALF, S, "3b")
+
+        h_ps = [psum.tile([P, S], F32, name="h_ps%d" % t) for t in range(PACK)]
+        hc = [sb("hc%d" % t, [P, S], F32) for t in range(PACK)]
+
+        def second_product(u, tag):
+            cols = slice(u * HALF, (u + 1) * HALF)
+            z_b = sb("z_b%d" % u, [P, HALF, PACK], BF16)
+            nc.scalar.copy(
+                z_b[:].rearrange("p (c i) t -> p c t i", i=4),
+                z_planes[:, :, cols].rearrange("p t (c i) -> p c t i", i=4),
+            )
+            z_c = sb("z_c%d" % u, [P, HALF], U32, tag=tag)
+            z_s = sb("z_s%d" % u, [P, HALF], U8)
+            nc.vector.quantize_mx(
+                out=z_c[:].bitcast(FP8X4), scales=z_s[:], in_=z_b[:].rearrange("p j t -> p (j t)")
+            )
+            for t in range(PACK):
+                nc.tensor.matmul_mx(
+                    out=h_ps[t][:, cols],
+                    lhsT=w2_c[:, t * P : (t + 1) * P].bitcast(FP8X4),
+                    lhsT_scale=w2_s[:, t * P : (t + 1) * P],
+                    rhs=z_c[:].bitcast(FP8X4),
+                    rhs_scale=z_s[:],
+                    start=True,
+                    stop=True,
+                )
+
+        def negated_h(t, lo, hi):
+            nc.scalar.activation(win[t][:, lo:hi], h_ps[t][:, lo:hi], ACT.Copy, scale=-1.0)
+            nc.scalar.activation(hc[t][:, lo:hi], h_ps[t][:, lo:hi], ACT.Copy, scale=-1.0)
+
+        second_product(0, "d_3b")
+        negated_h(0, 0, HALF)
+        denominator(2, "z_b0")
+        second_product(1, "acopy2")
+        denominator(3, "z_b1")
+        negated_h(0, HALF, S)
+        negated_h(1, 0, S)
+        reciprocal(2)
+        negated_h(2, 0, S)
+        reciprocal(3)
+        negated_h(3, 0, S)
+
+        out_rows = out.rearrange("(p t) j -> p t j", t=PACK)
+
+        def finish(t, lo, hi, name, tag=None):
+            e = sb("e" + name, [P, hi - lo], F32, tag=tag)
+            res = sb("res" + name, [P, hi - lo], F32)
+            nc.vector.tensor_tensor(e[:], win[t][:].indirect(entries("n3", lo, hi)), hc[t][:, lo:hi], ALU.subtract)
+            nc.vector.tensor_tensor(res[:], e[:], recip[t][:, lo:hi], ALU.mult)
+            nc.sync.dma_start(out_rows[:, t, lo:hi], res[:])
+
+        finish(0, 0, S, "0", tag="acopy3")
+        finish(1, 0, S, "1")
+        finish(2, 0, S, "2")
+        finish(3, 0, HALF, "3a")
+        finish(3, HALF, S, "3b")

@@ -87,7 +87,7 @@ def tile_picked_skipnormbwind_none_p_kernel(
                 raw[:].rearrange("p j (m t) -> p m j t", t=PACK)[:, m0 - raw_m0 : m1 - raw_m0],
             )
 
-        w1_b = sb("w1_b", [P, PACK, P, PACK], BF16)
+        w1_b = sb("w1_b", [P, PACK, P, PACK], BF16, tag="xs")
         deal(nc.scalar.copy, w1_b, w1_raw[0], 0, 64, 0)
         deal(nc.vector.tensor_copy, w1_b, w1_raw[1], 64, 112, 64)
         deal(nc.scalar.copy, w1_b, w1_raw[1], 112, 128, 64)
@@ -110,30 +110,47 @@ def tile_picked_skipnormbwind_none_p_kernel(
                 stop=True,
             )
 
-        for t in range(PACK):
+        y_sb = [sb("y_sb%d" % t, [P, S], F32) for t in range(PACK - 1)]
+        acopy = [sb("acopy%d" % t, [P, S], F32) for t in range(PACK)]
+
+        def gained_y(t):
             nc.scalar.activation(win[t][:, :S], y_ps[t][:], ACT.Copy, scale=gain[:, t : t + 1])
 
-        acopy = [sb("acopy%d" % t, [P, S], F32) for t in range(PACK)]
+        def plain_y(t):
+            nc.scalar.copy(y_sb[t][:], y_ps[t][:])
 
         def size_of_y(t):
             nc.scalar.activation(awin[t][:, :S], y_ps[t][:], ACT.Abs)
             nc.sync.dma_start(acopy[t][:], awin[t][:, :S])
 
+        gained_y(0)
+        gained_y(1)
+        plain_y(0)
         size_of_y(0)
         size_of_y(1)
+        gained_y(2)
+        plain_y(1)
         w2_b = sb("w2_b", [P, PACK, P, PACK], BF16)
         deal(nc.scalar.copy, w2_b, w2_raw, 0, 128, 0)
+        gained_y(3)
+        plain_y(2)
         size_of_y(2)
         size_of_y(3)
 
         z_planes = sb("z_planes", [P, PACK, S], BF16)
+        g2 = {}
+
+        def second_neighbour(t):
+            g2[t] = sb("g2_%d" % t, [P, S], F32)
+            nc.vector.tensor_copy(g2[t][:], win[t][:].indirect(lists["n2"][:]))
 
         def z_plane(t, lo, hi, name, tag=None):
-            g2 = sb("g2_" + name, [P, hi - lo], F32, tag=tag)
-            d = sb("d_" + name, [P, hi - lo], F32)
-            nc.vector.tensor_copy(g2[:], win[t][:].indirect(entries("n2", lo, hi)))
-            nc.vector.tensor_tensor(d[:], win[t][:].indirect(entries("n1", lo, hi)), g2[:], ALU.subtract)
-            nc.vector.tensor_tensor(z_planes[:, t, lo:hi], d[:], y_ps[t][:, lo:hi], ALU.mult)
+            d = sb("d_" + name, [P, hi - lo], F32, tag=tag)
+            nc.vector.tensor_tensor(d[:], win[t][:].indirect(entries("n1", lo, hi)), g2[t][:, lo:hi], ALU.subtract)
+            if t < PACK - 1:
+                nc.gpsimd.tensor_tensor(z_planes[:, t, lo:hi], d[:], y_sb[t][:, lo:hi], ALU.mult)
+            else:
+                nc.vector.tensor_tensor(z_planes[:, t, lo:hi], d[:], y_ps[t][:, lo:hi], ALU.mult)
 
         den = {}
 
@@ -149,18 +166,22 @@ def tile_picked_skipnormbwind_none_p_kernel(
             nc.scalar.activation(root[:], den[t][:], ACT.Abs_reciprocal_sqrt, bias=0.5)
             nc.scalar.activation(recip[t][:], root[:], ACT.Square)
 
+        second_neighbour(0)
         z_plane(0, 0, S, "0")
+        second_neighbour(1)
         z_plane(1, 0, S, "1")
-        w2_c = sb("w2_c", [P, N], U32)
-        w2_s = sb("w2_s", [P, N], U8)
+        second_neighbour(2)
         denominator(0, "d_1")
         reciprocal(0)
         denominator(1, "acopy0")
         reciprocal(1)
+        w2_c = sb("w2_c", [P, N], U32, tag="acopy1")
+        w2_s = sb("w2_s", [P, N], U8)
         nc.vector.quantize_mx(
             out=w2_c[:].bitcast(FP8X4), scales=w2_s[:], in_=w2_b[:].rearrange("p t m j -> p (t m j)")
         )
-        z_plane(2, 0, S, "2", tag="acopy1")
+        z_plane(2, 0, S, "2", tag="w2_b")
+        second_neighbour(3)
         z_plane(3, 0, HALF, "3a")
         z_plane(3, HALF, S, "3b")
 

@@ -40,125 +40,127 @@ def tile_picked_skipnormbwind_none_p_kernel(
             return lists[name][:, lo // 16 : hi // 16]
 
         xs = sb("xs", [P, T], U8)
-        nc.vector.memset(xs[:].bitcast(I32), 0)
+        for q in range(4):
+            rows = x_scales[0, 4 * q : 4 * q + 4, :].bitcast(I32)
+            nc.sync.dma_start(
+                xs[32 * q : 32 * q + 32, :].bitcast(I32),
+                rows.unsqueeze(0).broadcast_to([8, 4, T // 4]),
+            )
         nc.sync.dma_start(lists["offs"][:], offs)
+        w1_raw = sb("w1_raw", [P, PACK, H], F32)
+        nc.sync.dma_start(w1_raw[:], w1.rearrange("(p j) c -> p j c", j=PACK))
+        xw = sb("xw", [P, T], I32)
+        nc.sync.dma_start(xw[:], x_words[0].rearrange("p n t -> p (n t)").bitcast(I32))
         nc.sync.dma_start(lists["n2"][:], n2)
         nc.sync.dma_start(lists["n1"][:], n1)
+        gain = sb("gain", [P, PACK], F32)
+        nc.sync.dma_start(gain[:], gn.rearrange("(p t) o -> p (t o)", t=PACK))
+        w2_raw = sb("w2_raw", [P, PACK, N], F32)
+        nc.sync.dma_start(w2_raw[:], w2.rearrange("(p j) c -> p j c", j=PACK))
         nc.sync.dma_start(lists["n4"][:], n4)
-        xw = sb("xw", [P, T], I32, tag="big_load")
-        nc.sync.dma_start(xw[:], x_words[0].rearrange("p n t -> p (n t)").bitcast(I32))
-        half = H // 2
-        w1_raw = [sb("w1_raw%d" % u, [P, PACK, half], F32) for u in range(2)]
-        w1_rows = w1.rearrange("(p j) c -> p j c", j=PACK)
-        for u in range(2):
-            nc.sync.dma_start(w1_raw[u][:], w1_rows[:, :, u * half : (u + 1) * half])
         nc.sync.dma_start(lists["n3"][:], n3)
 
         warm = sb("warm", [P, 8], F32)
         warm2 = sb("warm2", [P, 8], F32)
         nc.vector.memset(warm[:], 1.0)
         nc.scalar.activation(warm2[:], warm[:], ACT.Abs_reciprocal_sqrt)
-        for q in range(4):
-            nc.scalar.dma_start(
-                xs[32 * q : 32 * q + 4, :].bitcast(I32),
-                x_scales[0, 4 * q : 4 * q + 4, :].bitcast(I32),
-            )
-        gain = sb("gain", [P, PACK], F32)
-        nc.gpsimd.dma_start(gain[:], gn.rearrange("(p t) o -> p (t o)", t=PACK))
 
         win = [sb("win%d" % t, [P, WIN], F32) for t in range(PACK)]
         awin = [sb("awin%d" % t, [P, WIN], F32) for t in range(PACK)]
-        for t in range(PACK):
-            nc.vector.memset(win[t][:, S:], 0.0)
-        for t in range(PACK):
-            nc.gpsimd.memset(awin[t][:, S:], 0.0)
 
         xg_s = sb("xg_s", [P, S], U8)
         xg_w = sb("xg_w", [P, S], I32)
-        nc.vector.tensor_copy(xg_w[:].bitcast(U32), xw[:].bitcast(U32).indirect(lists["offs"][:]))
         nc.vector.tensor_copy(xg_s[:], xs[:].indirect(lists["offs"][:]))
 
-        w2_raw = sb("w2_raw", [P, PACK, N], F32, tag="big_load")
-        nc.sync.dma_start(w2_raw[:], w2.rearrange("(p j) c -> p j c", j=PACK))
-
-        def deal(engine_copy, grouped, raw, m0, m1, raw_m0):
+        def deal(engine_copy, grouped, raw, m0, m1):
             engine_copy(
-                grouped[:, :, m0:m1, :].rearrange("p t m j -> p m j t"),
-                raw[:].rearrange("p j (m t) -> p m j t", t=PACK)[:, m0 - raw_m0 : m1 - raw_m0],
+                grouped[:, :, m0:m1, :],
+                raw[:].rearrange("p j (m t) -> p t m j", t=PACK)[:, :, m0:m1, :],
             )
 
         w1_b = sb("w1_b", [P, PACK, P, PACK], BF16, tag="xs")
-        deal(nc.scalar.copy, w1_b, w1_raw[0], 0, 64, 0)
-        deal(nc.vector.tensor_copy, w1_b, w1_raw[1], 64, 112, 64)
-        deal(nc.scalar.copy, w1_b, w1_raw[1], 112, 128, 64)
-        w1_c = sb("w1_c", [P, PACK, P], U32)
-        w1_s = sb("w1_s", [P, PACK, P], U8)
-        y_ps = [psum.tile([P, S], F32, name="y_ps%d" % t) for t in range(PACK)]
-        for t in range(PACK):
-            nc.vector.quantize_mx(
-                out=w1_c[:, t, :].bitcast(FP8X4),
-                scales=w1_s[:, t, :],
-                in_=w1_b[:, t].rearrange("p m j -> p (m j)"),
+        deal(nc.vector.tensor_copy, w1_b, w1_raw, 0, 88)
+        deal(nc.scalar.copy, w1_b, w1_raw, 88, P)
+        w1_c = sb("w1_c", [P, PACK * P], U32)
+        w1_s = sb("w1_s", [P, PACK * P], U8)
+        nc.vector.quantize_mx(
+            out=w1_c[:].bitcast(FP8X4), scales=w1_s[:], in_=w1_b[:].rearrange("p t m j -> p (t m j)")
+        )
+        for lo in (0, HALF):
+            nc.vector.tensor_copy(
+                xg_w[:, lo : lo + HALF].bitcast(U32),
+                xw[:].bitcast(U32).indirect(entries("offs", lo, lo + HALF)),
             )
+
+        def product(bank, codes, scales, t, moving, moving_scales):
             nc.tensor.matmul_mx(
-                out=y_ps[t][:],
-                lhsT=w1_c[:, t, :].bitcast(FP8X4),
-                lhsT_scale=w1_s[:, t, :],
-                rhs=xg_w[:].bitcast(FP8X4),
-                rhs_scale=xg_s[:],
+                out=bank,
+                lhsT=codes[:, t * P : (t + 1) * P].bitcast(FP8X4),
+                lhsT_scale=scales[:, t * P : (t + 1) * P],
+                rhs=moving.bitcast(FP8X4),
+                rhs_scale=moving_scales,
                 start=True,
                 stop=True,
             )
 
-        y_sb = [sb("y_sb%d" % t, [P, S], F32) for t in range(PACK - 1)]
+        y_parts = {}
+        early = psum.tile([P, S], F32, name="y_early", tag="h_ps3")
+        y_ps = [psum.tile([P, S], F32, name="y_ps%d" % t) for t in range(PACK)]
+        y_parts[0] = [(0, HALF, early[:, :HALF]), (HALF, S, y_ps[0][:, :HALF])]
+        for t in range(1, PACK):
+            y_parts[t] = [(0, S, y_ps[t][:])]
+        for t in range(PACK):
+            for lo, hi, bank in y_parts[t]:
+                product(bank, w1_c, w1_s, t, xg_w[:, lo:hi], xg_s[:, lo:hi])
+
         acopy = [sb("acopy%d" % t, [P, S], F32) for t in range(PACK)]
 
         def gained_y(t):
-            nc.scalar.activation(win[t][:, :S], y_ps[t][:], ACT.Copy, scale=gain[:, t : t + 1])
-
-        def plain_y(t):
-            nc.scalar.copy(y_sb[t][:], y_ps[t][:])
+            for lo, hi, bank in y_parts[t]:
+                nc.scalar.activation(win[t][:, lo:hi], bank, ACT.Copy, scale=gain[:, t : t + 1])
 
         def size_of_y(t):
-            nc.scalar.activation(awin[t][:, :S], y_ps[t][:], ACT.Abs)
+            for lo, hi, bank in y_parts[t]:
+                nc.scalar.activation(awin[t][:, lo:hi], bank, ACT.Abs)
             nc.sync.dma_start(acopy[t][:], awin[t][:, :S])
 
         gained_y(0)
         gained_y(1)
-        plain_y(0)
-        size_of_y(0)
-        size_of_y(1)
         gained_y(2)
-        plain_y(1)
-        w2_b = sb("w2_b", [P, PACK, P, PACK], BF16)
-        deal(nc.scalar.copy, w2_b, w2_raw, 0, 128, 0)
+        size_of_y(0)
         gained_y(3)
-        plain_y(2)
+        size_of_y(1)
+        w2_b = sb("w2_b", [P, PACK, P, PACK], BF16)
+        deal(nc.scalar.copy, w2_b, w2_raw, 0, P)
         size_of_y(2)
         size_of_y(3)
 
         z_planes = sb("z_planes", [P, PACK, S], BF16)
-        g2 = {}
+        g2, diff, den, recip = {}, {}, {}, {}
 
         def second_neighbour(t):
             g2[t] = sb("g2_%d" % t, [P, S], F32)
             nc.vector.tensor_copy(g2[t][:], win[t][:].indirect(lists["n2"][:]))
 
-        def z_plane(t, lo, hi, name, tag=None):
-            d = sb("d_" + name, [P, hi - lo], F32, tag=tag)
-            nc.vector.tensor_tensor(d[:], win[t][:].indirect(entries("n1", lo, hi)), g2[t][:, lo:hi], ALU.subtract)
-            if t < PACK - 1:
-                nc.gpsimd.tensor_tensor(z_planes[:, t, lo:hi], d[:], y_sb[t][:, lo:hi], ALU.mult)
-            else:
-                nc.vector.tensor_tensor(z_planes[:, t, lo:hi], d[:], y_ps[t][:, lo:hi], ALU.mult)
+        def difference(t, lo, hi, tag=None):
+            diff[t, lo] = sb("diff%d_%d" % (t, lo), [P, hi - lo], F32, tag=tag)
+            nc.vector.tensor_tensor(
+                diff[t, lo][:], win[t][:].indirect(entries("n1", lo, hi)), g2[t][:, lo:hi], ALU.subtract
+            )
 
-        den = {}
+        def z_plane(t, lo, hi):
+            for a, b, bank in y_parts[t]:
+                first, last = max(a, lo), min(b, hi)
+                nc.vector.tensor_tensor(
+                    z_planes[:, t, first:last],
+                    diff[t, lo][:, first - lo : last - lo],
+                    bank[:, first - a : last - a],
+                    ALU.mult,
+                )
 
         def denominator(t, tag):
             den[t] = sb("den%d" % t, [P, S], F32, tag=tag)
             nc.vector.tensor_tensor(den[t][:], awin[t][:].indirect(lists["n4"][:]), acopy[t][:], ALU.add)
-
-        recip = {}
 
         def reciprocal(t):
             root = sb("root%d" % t, [P, S], F32)
@@ -167,26 +169,31 @@ def tile_picked_skipnormbwind_none_p_kernel(
             nc.scalar.activation(recip[t][:], root[:], ACT.Square)
 
         second_neighbour(0)
-        z_plane(0, 0, S, "0")
         second_neighbour(1)
-        z_plane(1, 0, S, "1")
+        difference(0, 0, S)
         second_neighbour(2)
-        denominator(0, "d_1")
+        z_plane(0, 0, S)
+        difference(1, 0, S)
+        second_neighbour(3)
+        z_plane(1, 0, S)
+        difference(2, 0, S)
+        denominator(0, "diff1_0")
         reciprocal(0)
-        denominator(1, "acopy0")
+        z_plane(2, 0, S)
+        difference(3, 0, HALF, tag="acopy0")
+        denominator(1, None)
         reciprocal(1)
-        w2_c = sb("w2_c", [P, N], U32, tag="acopy1")
+        z_plane(3, 0, HALF)
+        difference(3, HALF, S, tag="acopy0")
+        w2_c = sb("w2_c", [P, N], U32, tag="g2_3")
         w2_s = sb("w2_s", [P, N], U8)
         nc.vector.quantize_mx(
             out=w2_c[:].bitcast(FP8X4), scales=w2_s[:], in_=w2_b[:].rearrange("p t m j -> p (t m j)")
         )
-        z_plane(2, 0, S, "2", tag="w2_b")
-        second_neighbour(3)
-        z_plane(3, 0, HALF, "3a")
-        z_plane(3, HALF, S, "3b")
+        z_plane(3, HALF, S)
 
         h_ps = [psum.tile([P, S], F32, name="h_ps%d" % t) for t in range(PACK)]
-        hc = [sb("hc%d" % t, [P, S], F32) for t in range(PACK)]
+        hc = {}
 
         def second_product(u, tag):
             cols = slice(u * HALF, (u + 1) * HALF)
@@ -201,43 +208,54 @@ def tile_picked_skipnormbwind_none_p_kernel(
                 out=z_c[:].bitcast(FP8X4), scales=z_s[:], in_=z_b[:].rearrange("p j t -> p (j t)")
             )
             for t in range(PACK):
-                nc.tensor.matmul_mx(
-                    out=h_ps[t][:, cols],
-                    lhsT=w2_c[:, t * P : (t + 1) * P].bitcast(FP8X4),
-                    lhsT_scale=w2_s[:, t * P : (t + 1) * P],
-                    rhs=z_c[:].bitcast(FP8X4),
-                    rhs_scale=z_s[:],
-                    start=True,
-                    stop=True,
-                )
+                product(h_ps[t][:, cols], w2_c, w2_s, t, z_c[:], z_s[:])
 
         def negated_h(t, lo, hi):
             nc.scalar.activation(win[t][:, lo:hi], h_ps[t][:, lo:hi], ACT.Copy, scale=-1.0)
-            nc.scalar.activation(hc[t][:, lo:hi], h_ps[t][:, lo:hi], ACT.Copy, scale=-1.0)
 
-        second_product(0, "d_3b")
+        def negated_h_copy(t, lo, hi):
+            hc[t, lo] = sb("hc%d_%d" % (t, lo), [P, hi - lo], F32)
+            nc.scalar.activation(hc[t, lo][:], h_ps[t][:, lo:hi], ACT.Copy, scale=-1.0)
+
+        second_product(0, "acopy0")
+        hc[0, 0] = sb("hc0_0", [P, S], F32)
         negated_h(0, 0, HALF)
+        nc.scalar.activation(hc[0, 0][:, :HALF], h_ps[0][:, :HALF], ACT.Copy, scale=-1.0)
         denominator(2, "z_b0")
         second_product(1, "acopy2")
         denominator(3, "z_b1")
         negated_h(0, HALF, S)
-        negated_h(1, 0, S)
+        nc.scalar.activation(hc[0, 0][:, HALF:], h_ps[0][:, HALF:], ACT.Copy, scale=-1.0)
+        for t in (1, 2):
+            negated_h(t, 0, S)
+            negated_h_copy(t, 0, S)
         reciprocal(2)
-        negated_h(2, 0, S)
-        reciprocal(3)
         negated_h(3, 0, S)
+        negated_h_copy(3, 0, HALF)
+        negated_h_copy(3, HALF, S)
+        reciprocal(3)
 
         out_rows = out.rearrange("(p t) j -> p t j", t=PACK)
+        numer = {}
 
-        def finish(t, lo, hi, name, tag=None):
-            e = sb("e" + name, [P, hi - lo], F32, tag=tag)
-            res = sb("res" + name, [P, hi - lo], F32)
-            nc.vector.tensor_tensor(e[:], win[t][:].indirect(entries("n3", lo, hi)), hc[t][:, lo:hi], ALU.subtract)
-            nc.vector.tensor_tensor(res[:], e[:], recip[t][:, lo:hi], ALU.mult)
+        def numerator(t, lo, hi, tag=None):
+            numer[t, lo] = sb("numer%d_%d" % (t, lo), [P, hi - lo], F32, tag=tag)
+            nc.vector.tensor_tensor(
+                numer[t, lo][:], win[t][:].indirect(entries("n3", lo, hi)), hc[t, lo][:], ALU.subtract
+            )
+
+        def finish(t, lo, hi, tag=None):
+            res = sb("res%d_%d" % (t, lo), [P, hi - lo], F32, tag=tag)
+            nc.vector.tensor_tensor(res[:], numer[t, lo][:], recip[t][:, lo:hi], ALU.mult)
             nc.sync.dma_start(out_rows[:, t, lo:hi], res[:])
 
-        finish(0, 0, S, "0", tag="acopy3")
-        finish(1, 0, S, "1")
-        finish(2, 0, S, "2")
-        finish(3, 0, HALF, "3a")
-        finish(3, HALF, S, "3b")
+        numerator(0, 0, S, tag="acopy3")
+        numerator(1, 0, S)
+        finish(0, 0, S, tag="hc1_0")
+        numerator(2, 0, S)
+        finish(1, 0, S, tag="hc2_0")
+        numerator(3, 0, HALF)
+        finish(2, 0, S, tag="hc3_0")
+        numerator(3, HALF, S)
+        finish(3, 0, HALF, tag="hc3_%d" % HALF)
+        finish(3, HALF, S)

@@ -1,6 +1,7 @@
 from contextlib import ExitStack
 
 import concourse.mybir as mybir
+from concourse.masks import make_identity
 
 K, T, S, N, H = 512, 2048, 512, 512, 512
 FLOPS = 2 * K * H * S + 2 * H * N * S
@@ -17,8 +18,11 @@ ACT = mybir.ActivationFunctionType
 
 P = 128
 PACK = 4
-WIN = 2 * S
 HALF = S // 2
+WINDOW = 2 * S
+LAST = PACK - 1
+SCALAR_PLANES = (0, 1)
+VECTOR_PLANES = (2, 3)
 
 
 def tile_picked_skipnormbwind_none_p_kernel(
@@ -29,8 +33,8 @@ def tile_picked_skipnormbwind_none_p_kernel(
         keep = ctx.enter_context(tc.tile_pool(name="keep", bufs=1))
         psum = ctx.enter_context(tc.psum_pool(name="psum", bufs=1))
 
-        def sb(name, shape, dtype, tag=None):
-            return keep.tile(shape, dtype, name=name, tag=tag or name, align_bytes=64)
+        def sb(name, shape, dtype, after=None):
+            return keep.tile(shape, dtype, name=name, tag=after or name, align_bytes=64)
 
         lists = {}
         for name in ("offs", "n1", "n2", "n3", "n4"):
@@ -39,18 +43,18 @@ def tile_picked_skipnormbwind_none_p_kernel(
         def entries(name, lo, hi):
             return lists[name][:, lo // 16 : hi // 16]
 
-        xs = sb("xs", [P, T], U8)
+        x_bytes = sb("x_bytes", [P, T], U8)
         for q in range(4):
             rows = x_scales[0, 4 * q : 4 * q + 4, :].bitcast(I32)
             nc.sync.dma_start(
-                xs[32 * q : 32 * q + 32, :].bitcast(I32),
+                x_bytes[32 * q : 32 * q + 32, :].bitcast(I32),
                 rows.unsqueeze(0).broadcast_to([8, 4, T // 4]),
             )
         nc.sync.dma_start(lists["offs"][:], offs)
         w1_raw = sb("w1_raw", [P, PACK, H], F32)
         nc.sync.dma_start(w1_raw[:], w1.rearrange("(p j) c -> p j c", j=PACK))
-        xw = sb("xw", [P, T], I32)
-        nc.sync.dma_start(xw[:], x_words[0].rearrange("p n t -> p (n t)").bitcast(I32))
+        x_codes = sb("x_codes", [P, T], I32)
+        nc.sync.dma_start(x_codes[:], x_words[0].rearrange("p n t -> p (n t)").bitcast(I32))
         nc.sync.dma_start(lists["n2"][:], n2)
         nc.sync.dma_start(lists["n1"][:], n1)
         gain = sb("gain", [P, PACK], F32)
@@ -60,69 +64,68 @@ def tile_picked_skipnormbwind_none_p_kernel(
         nc.sync.dma_start(lists["n4"][:], n4)
         nc.sync.dma_start(lists["n3"][:], n3)
 
-        warm = sb("warm", [P, 8], F32)
-        warm2 = sb("warm2", [P, 8], F32)
-        nc.vector.memset(warm[:], 1.0)
-        nc.scalar.activation(warm2[:], warm[:], ACT.Abs_reciprocal_sqrt)
+        preload_in = sb("preload_in", [P, 8], F32)
+        preload_out = sb("preload_out", [P, 8], F32)
+        nc.vector.memset(preload_in[:], 1.0)
+        nc.scalar.activation(preload_out[:], preload_in[:], ACT.Ln)
+        ident = sb("ident", [P, P], F32)
+        make_identity(nc, ident[:])
 
-        win = [sb("win%d" % t, [P, WIN], F32) for t in range(PACK)]
-        awin = [sb("awin%d" % t, [P, WIN], F32) for t in range(PACK)]
+        picked_bytes = sb("picked_bytes", [P, S], U8)
+        picked_codes = sb("picked_codes", [P, S], I32)
+        nc.vector.tensor_copy(picked_bytes[:], x_bytes[:].indirect(lists["offs"][:]))
 
-        xg_s = sb("xg_s", [P, S], U8)
-        xg_w = sb("xg_w", [P, S], I32)
-        nc.vector.tensor_copy(xg_s[:], xs[:].indirect(lists["offs"][:]))
+        w1_cols = w1_raw[:].rearrange("p j (m t) -> p t m j", t=PACK)
+        w1_bf = [sb("w1_bf%d" % u, [P, 2, P, PACK], BF16, after=("x_bytes", None)[u]) for u in range(2)]
+        nc.vector.tensor_copy(w1_bf[0][:], w1_cols[:, 0:2])
+        nc.scalar.copy(w1_bf[1][:], w1_cols[:, 2:4])
 
-        def deal(engine_copy, grouped, raw, m0, m1):
-            engine_copy(
-                grouped[:, :, m0:m1, :],
-                raw[:].rearrange("p j (m t) -> p t m j", t=PACK)[:, :, m0:m1, :],
-            )
+        def quantise(name, source, width, after=None):
+            codes = sb(name + "_codes", [P, width], U32, after=after)
+            scales = sb(name + "_scales", [P, width], U8)
+            nc.vector.quantize_mx(out=codes[:].bitcast(FP8X4), scales=scales[:], in_=source)
+            return codes, scales
 
-        w1_b = sb("w1_b", [P, PACK, P, PACK], BF16, tag="xs")
-        deal(nc.vector.tensor_copy, w1_b, w1_raw, 0, 88)
-        deal(nc.scalar.copy, w1_b, w1_raw, 88, P)
-        w1_c = sb("w1_c", [P, PACK * P], U32)
-        w1_s = sb("w1_s", [P, PACK * P], U8)
-        nc.vector.quantize_mx(
-            out=w1_c[:].bitcast(FP8X4), scales=w1_s[:], in_=w1_b[:].rearrange("p t m j -> p (t m j)")
-        )
-        for lo in (0, HALF):
-            nc.vector.tensor_copy(
-                xg_w[:, lo : lo + HALF].bitcast(U32),
-                xw[:].bitcast(U32).indirect(entries("offs", lo, lo + HALF)),
-            )
-
-        def product(bank, codes, scales, t, moving, moving_scales):
+        def product(bank, stationary, block, moving_codes, moving_scales):
+            codes, scales = stationary
             nc.tensor.matmul_mx(
                 out=bank,
-                lhsT=codes[:, t * P : (t + 1) * P].bitcast(FP8X4),
-                lhsT_scale=scales[:, t * P : (t + 1) * P],
-                rhs=moving.bitcast(FP8X4),
+                lhsT=codes[:, block * P : (block + 1) * P].bitcast(FP8X4),
+                lhsT_scale=scales[:, block * P : (block + 1) * P],
+                rhs=moving_codes.bitcast(FP8X4),
                 rhs_scale=moving_scales,
                 start=True,
                 stop=True,
             )
 
-        y_parts = {}
-        early = psum.tile([P, S], F32, name="y_early", tag="h_ps3")
+        w1_mx = [quantise("w1_lo", w1_bf[0][:].rearrange("p t m j -> p (t m j)"), 2 * P)]
+        for lo in (0, HALF):
+            nc.vector.tensor_copy(
+                picked_codes[:, lo : lo + HALF].bitcast(U32),
+                x_codes[:].bitcast(U32).indirect(entries("offs", lo, lo + HALF)),
+            )
+        w1_mx.append(quantise("w1_hi", w1_bf[1][:].rearrange("p t m j -> p (t m j)"), 2 * P, after="x_codes"))
+
+        y_first_half = psum.tile([P, S], F32, name="y_first_half", tag="h_ps%d" % LAST)
         y_ps = [psum.tile([P, S], F32, name="y_ps%d" % t) for t in range(PACK)]
-        y_parts[0] = [(0, HALF, early[:, :HALF]), (HALF, S, y_ps[0][:, :HALF])]
+        y_parts = {0: [(0, HALF, y_first_half[:, :HALF]), (HALF, S, y_ps[0][:, :HALF])]}
         for t in range(1, PACK):
             y_parts[t] = [(0, S, y_ps[t][:])]
         for t in range(PACK):
             for lo, hi, bank in y_parts[t]:
-                product(bank, w1_c, w1_s, t, xg_w[:, lo:hi], xg_s[:, lo:hi])
+                product(bank, w1_mx[t // 2], t % 2, picked_codes[:, lo:hi], picked_bytes[:, lo:hi])
 
-        acopy = [sb("acopy%d" % t, [P, S], F32) for t in range(PACK)]
+        looked_up = [sb("looked_up%d" % t, [P, WINDOW], F32) for t in range(PACK)]
+        size = [sb("size%d" % t, [P, WINDOW], F32) for t in range(PACK)]
+        size_copy = {t: sb("size_copy%d" % t, [P, S], F32) for t in VECTOR_PLANES}
 
         def gained_y(t):
             for lo, hi, bank in y_parts[t]:
-                nc.scalar.activation(win[t][:, lo:hi], bank, ACT.Copy, scale=gain[:, t : t + 1])
+                nc.scalar.activation(looked_up[t][:, lo:hi], bank, ACT.Copy, scale=gain[:, t : t + 1])
 
         def size_of_y(t):
             for lo, hi, bank in y_parts[t]:
-                nc.scalar.activation(awin[t][:, lo:hi], bank, ACT.Abs)
-            nc.sync.dma_start(acopy[t][:], awin[t][:, :S])
+                nc.scalar.activation(size[t][:, lo:hi], bank, ACT.Abs)
 
         gained_y(0)
         gained_y(1)
@@ -130,132 +133,154 @@ def tile_picked_skipnormbwind_none_p_kernel(
         size_of_y(0)
         gained_y(3)
         size_of_y(1)
-        w2_b = sb("w2_b", [P, PACK, P, PACK], BF16)
-        deal(nc.scalar.copy, w2_b, w2_raw, 0, P)
-        size_of_y(2)
-        size_of_y(3)
+        log_size = {t: sb("log_size%d" % t, [P, WINDOW], F32) for t in SCALAR_PLANES}
+        far_size = {t: sb("far_size%d" % t, [P, S], F32) for t in SCALAR_PLANES}
+        for t in SCALAR_PLANES:
+            nc.scalar.activation(log_size[t][:, :S], size[t][:, :S], ACT.Ln, bias=0.25)
+        for t in SCALAR_PLANES:
+            nc.scalar.activation(far_size[t][:], log_size[t][:].indirect(lists["n4"][:]), ACT.Exp)
+        for t in VECTOR_PLANES:
+            size_of_y(t)
+            nc.sync.dma_start(size_copy[t][:], size[t][:, :S])
+        w2_bf = sb("w2_bf", [P, PACK, P, PACK], BF16)
+        nc.scalar.copy(
+            w2_bf[:].rearrange("p t m j -> p m j t"), w2_raw[:].rearrange("p j (m t) -> p m j t", t=PACK)
+        )
 
         z_planes = sb("z_planes", [P, PACK, S], BF16)
-        g2, diff, den, recip = {}, {}, {}, {}
+        at_n2, diff, den, root, recip = {}, {}, {}, {}, {}
 
-        def second_neighbour(t):
-            g2[t] = sb("g2_%d" % t, [P, S], F32)
-            nc.vector.tensor_copy(g2[t][:], win[t][:].indirect(lists["n2"][:]))
+        def fetch_n2(t):
+            at_n2[t] = sb("at_n2_%d" % t, [P, S], F32)
+            nc.vector.tensor_copy(at_n2[t][:], looked_up[t][:].indirect(lists["n2"][:]))
 
-        def difference(t, lo, hi, tag=None):
-            diff[t, lo] = sb("diff%d_%d" % (t, lo), [P, hi - lo], F32, tag=tag)
+        def difference(t, lo, hi, after=None):
+            diff[t, lo] = sb("diff%d_%d" % (t, lo), [P, hi - lo], F32, after=after)
             nc.vector.tensor_tensor(
-                diff[t, lo][:], win[t][:].indirect(entries("n1", lo, hi)), g2[t][:, lo:hi], ALU.subtract
+                diff[t, lo][:], looked_up[t][:].indirect(entries("n1", lo, hi)), at_n2[t][:, lo:hi], ALU.subtract
             )
 
         def z_plane(t, lo, hi):
             for a, b, bank in y_parts[t]:
-                first, last = max(a, lo), min(b, hi)
+                first, end = max(a, lo), min(b, hi)
                 nc.vector.tensor_tensor(
-                    z_planes[:, t, first:last],
-                    diff[t, lo][:, first - lo : last - lo],
-                    bank[:, first - a : last - a],
+                    z_planes[:, t, first:end],
+                    diff[t, lo][:, first - lo : end - lo],
+                    bank[:, first - a : end - a],
                     ALU.mult,
                 )
 
-        def denominator(t, tag):
-            den[t] = sb("den%d" % t, [P, S], F32, tag=tag)
-            nc.vector.tensor_tensor(den[t][:], awin[t][:].indirect(lists["n4"][:]), acopy[t][:], ALU.add)
-
-        def reciprocal(t):
-            root = sb("root%d" % t, [P, S], F32)
-            recip[t] = sb("recip%d" % t, [P, S], F32)
-            nc.scalar.activation(root[:], den[t][:], ACT.Abs_reciprocal_sqrt, bias=0.5)
-            nc.scalar.activation(recip[t][:], root[:], ACT.Square)
-
-        second_neighbour(0)
-        second_neighbour(1)
+        fetch_n2(0)
+        fetch_n2(1)
         difference(0, 0, S)
-        second_neighbour(2)
+        fetch_n2(2)
         z_plane(0, 0, S)
         difference(1, 0, S)
-        second_neighbour(3)
+        fetch_n2(3)
         z_plane(1, 0, S)
         difference(2, 0, S)
-        denominator(0, "diff1_0")
-        reciprocal(0)
+        difference(LAST, 0, HALF, after="last_plane")
         z_plane(2, 0, S)
-        difference(3, 0, HALF, tag="acopy0")
-        denominator(1, None)
-        reciprocal(1)
-        z_plane(3, 0, HALF)
-        difference(3, HALF, S, tag="acopy0")
-        w2_c = sb("w2_c", [P, N], U32, tag="g2_3")
-        w2_s = sb("w2_s", [P, N], U8)
-        nc.vector.quantize_mx(
-            out=w2_c[:].bitcast(FP8X4), scales=w2_s[:], in_=w2_b[:].rearrange("p t m j -> p (t m j)")
-        )
-        z_plane(3, HALF, S)
+        z_plane(LAST, 0, HALF)
+        difference(LAST, HALF, S, after="last_plane")
+
+        for t in SCALAR_PLANES:
+            den[t] = psum.tile([P, S], F32, name="den_turned%d" % t, tag="y_ps%d" % t)
+            for c in range(S // P):
+                cols = slice(c * P, (c + 1) * P)
+                nc.tensor.matmul(den[t][:, cols], size[t][:, cols], ident[:], start=True, stop=False, is_transpose=True)
+                nc.tensor.matmul(den[t][:, cols], far_size[t][:, cols], ident[:], start=False, stop=True, is_transpose=True)
+
+        w2_mx = quantise("w2", w2_bf[:].rearrange("p t m j -> p (t m j)"), N, after="at_n2_%d" % LAST)
+        z_plane(LAST, HALF, S)
 
         h_ps = [psum.tile([P, S], F32, name="h_ps%d" % t) for t in range(PACK)]
-        hc = {}
 
-        def second_product(u, tag):
+        def second_product(u, after):
             cols = slice(u * HALF, (u + 1) * HALF)
-            z_b = sb("z_b%d" % u, [P, HALF, PACK], BF16)
+            z_words = sb("z_words%d" % u, [P, HALF, PACK], BF16)
             nc.scalar.copy(
-                z_b[:].rearrange("p (c i) t -> p c t i", i=4),
+                z_words[:].rearrange("p (c i) t -> p c t i", i=4),
                 z_planes[:, :, cols].rearrange("p t (c i) -> p c t i", i=4),
             )
-            z_c = sb("z_c%d" % u, [P, HALF], U32, tag=tag)
-            z_s = sb("z_s%d" % u, [P, HALF], U8)
-            nc.vector.quantize_mx(
-                out=z_c[:].bitcast(FP8X4), scales=z_s[:], in_=z_b[:].rearrange("p j t -> p (j t)")
-            )
+            codes, scales = quantise("z%d" % u, z_words[:].rearrange("p j t -> p (j t)"), HALF, after=after)
             for t in range(PACK):
-                product(h_ps[t][:, cols], w2_c, w2_s, t, z_c[:], z_s[:])
+                product(h_ps[t][:, cols], w2_mx, t, codes[:], scales[:])
 
-        def negated_h(t, lo, hi):
-            nc.scalar.activation(win[t][:, lo:hi], h_ps[t][:, lo:hi], ACT.Copy, scale=-1.0)
+        def denominator(t, after):
+            den[t] = sb("den%d" % t, [P, S], F32, after=after)
+            nc.vector.tensor_tensor(den[t][:], size[t][:].indirect(lists["n4"][:]), size_copy[t][:], ALU.add)
 
-        def negated_h_copy(t, lo, hi):
-            hc[t, lo] = sb("hc%d_%d" % (t, lo), [P, hi - lo], F32)
-            nc.scalar.activation(hc[t, lo][:], h_ps[t][:, lo:hi], ACT.Copy, scale=-1.0)
+        second_product(0, after="last_plane")
+        denominator(2, after="z_words0")
+        second_product(1, after="size_copy2")
+        denominator(3, after="z_words1")
 
-        second_product(0, "acopy0")
-        hc[0, 0] = sb("hc0_0", [P, S], F32)
-        negated_h(0, 0, HALF)
-        nc.scalar.activation(hc[0, 0][:, :HALF], h_ps[0][:, :HALF], ACT.Copy, scale=-1.0)
-        denominator(2, "z_b0")
-        second_product(1, "acopy2")
-        denominator(3, "z_b1")
-        negated_h(0, HALF, S)
-        nc.scalar.activation(hc[0, 0][:, HALF:], h_ps[0][:, HALF:], ACT.Copy, scale=-1.0)
-        for t in (1, 2):
-            negated_h(t, 0, S)
-            negated_h_copy(t, 0, S)
-        reciprocal(2)
-        negated_h(3, 0, S)
-        negated_h_copy(3, 0, HALF)
-        negated_h_copy(3, HALF, S)
-        reciprocal(3)
+        minus_h = {}
+
+        def leave_psum(t):
+            nc.scalar.activation(looked_up[t][:, :S], h_ps[t][:], ACT.Copy, scale=-1.0)
+
+        def second_copy(t, lo, hi):
+            minus_h[t, lo] = sb("minus_h%d_%d" % (t, lo), [P, hi - lo], F32)
+            nc.scalar.activation(minus_h[t, lo][:], h_ps[t][:, lo:hi], ACT.Copy, scale=-1.0)
+
+        def turned_root(t, lo, hi):
+            nc.scalar.activation(root[t][:, lo:hi], den[t][:, lo:hi], ACT.Abs_reciprocal_sqrt, bias=0.25)
+
+        def turned_reciprocal(t):
+            back = psum.tile([P, S], F32, name="root_back%d" % t, tag="y_ps%d" % t)
+            for c in range(S // P):
+                cols = slice(c * P, (c + 1) * P)
+                nc.tensor.transpose(back[:, cols], root[t][:, cols], ident[:])
+            recip[t] = sb("recip%d" % t, [P, S], F32)
+            nc.scalar.activation(recip[t][:], back[:], ACT.Square)
+
+        def plain_reciprocal(t):
+            root[t] = sb("root%d" % t, [P, S], F32)
+            recip[t] = sb("recip%d" % t, [P, S], F32)
+            nc.scalar.activation(root[t][:], den[t][:], ACT.Abs_reciprocal_sqrt, bias=0.5)
+            nc.scalar.activation(recip[t][:], root[t][:], ACT.Square)
+
+        root[0] = sb("root0", [P, S], F32, after="z_planes")
+        turned_root(0, 0, P)
+        for t in (0, 1):
+            leave_psum(t)
+            second_copy(t, 0, S)
+        turned_root(0, P, S)
+        leave_psum(2)
+        second_copy(2, 0, S)
+        turned_reciprocal(0)
+        root[1] = sb("root1", [P, S], F32)
+        turned_root(1, 0, S)
+        leave_psum(LAST)
+        turned_reciprocal(1)
+        second_copy(LAST, 0, HALF)
+        second_copy(LAST, HALF, S)
+        for t in VECTOR_PLANES:
+            plain_reciprocal(t)
 
         out_rows = out.rearrange("(p t) j -> p t j", t=PACK)
         numer = {}
 
-        def numerator(t, lo, hi, tag=None):
-            numer[t, lo] = sb("numer%d_%d" % (t, lo), [P, hi - lo], F32, tag=tag)
+        def numerator(t, lo, hi, after=None):
+            numer[t, lo] = sb("numer%d_%d" % (t, lo), [P, hi - lo], F32, after=after)
             nc.vector.tensor_tensor(
-                numer[t, lo][:], win[t][:].indirect(entries("n3", lo, hi)), hc[t, lo][:], ALU.subtract
+                numer[t, lo][:], looked_up[t][:].indirect(entries("n3", lo, hi)), minus_h[t, lo][:], ALU.subtract
             )
 
-        def finish(t, lo, hi, tag=None):
-            res = sb("res%d_%d" % (t, lo), [P, hi - lo], F32, tag=tag)
-            nc.vector.tensor_tensor(res[:], numer[t, lo][:], recip[t][:, lo:hi], ALU.mult)
-            nc.sync.dma_start(out_rows[:, t, lo:hi], res[:])
+        def finish(t, lo, hi, after=None):
+            result = sb("result%d_%d" % (t, lo), [P, hi - lo], F32, after=after)
+            nc.vector.tensor_tensor(result[:], numer[t, lo][:], recip[t][:, lo:hi], ALU.mult)
+            nc.sync.dma_start(out_rows[:, t, lo:hi], result[:])
 
-        numerator(0, 0, S, tag="acopy3")
+        numerator(0, 0, S, after="size_copy3")
         numerator(1, 0, S)
-        finish(0, 0, S, tag="hc1_0")
         numerator(2, 0, S)
-        finish(1, 0, S, tag="hc2_0")
-        numerator(3, 0, HALF)
-        finish(2, 0, S, tag="hc3_0")
-        numerator(3, HALF, S)
-        finish(3, 0, HALF, tag="hc3_%d" % HALF)
-        finish(3, HALF, S)
+        finish(0, 0, S, after="minus_h2_0")
+        numerator(LAST, 0, HALF)
+        finish(1, 0, S, after="minus_h%d_0" % LAST)
+        numerator(LAST, HALF, S)
+        finish(2, 0, S, after="minus_h%d_%d" % (LAST, HALF))
+        finish(LAST, 0, HALF)
+        finish(LAST, HALF, S)

from contextlib import ExitStack

import concourse.mybir as mybir
from concourse.masks import make_identity

K, T, S, N, H = 512, 2048, 512, 512, 512
FLOPS = 2 * K * H * S + 2 * H * N * S

F32 = mybir.dt.float32
BF16 = mybir.dt.bfloat16
I32 = mybir.dt.int32
U32 = mybir.dt.uint32
U16 = mybir.dt.uint16
U8 = mybir.dt.uint8
FP8X4 = mybir.dt.float8_e4m3fn_x4
ALU = mybir.AluOpType
ACT = mybir.ActivationFunctionType

P = 128
PACK = 4
HALF = S // 2
WINDOW = 2 * S
LAST = PACK - 1
SCALAR_PLANES = (0, 1)
VECTOR_PLANES = (2, 3)


def tile_picked_skipnormbwind_none_p_kernel(
    tc, x_words, x_scales, w1, gn, w2, offs, n1, n2, n3, n4, out
):
    nc = tc.nc
    with ExitStack() as ctx:
        keep = ctx.enter_context(tc.tile_pool(name="keep", bufs=1))
        psum = ctx.enter_context(tc.psum_pool(name="psum", bufs=1))

        def sb(name, shape, dtype, after=None):
            return keep.tile(shape, dtype, name=name, tag=after or name, align_bytes=64)

        lists = {}
        for name in ("offs", "n1", "n2", "n3", "n4"):
            lists[name] = sb("list_" + name, [P, S // 16], U16)

        def entries(name, lo, hi):
            return lists[name][:, lo // 16 : hi // 16]

        x_bytes = sb("x_bytes", [P, T], U8)
        for q in range(4):
            rows = x_scales[0, 4 * q : 4 * q + 4, :].bitcast(I32)
            nc.sync.dma_start(
                x_bytes[32 * q : 32 * q + 32, :].bitcast(I32),
                rows.unsqueeze(0).broadcast_to([8, 4, T // 4]),
            )
        nc.sync.dma_start(lists["offs"][:], offs)
        w1_raw = sb("w1_raw", [P, PACK, H], F32)
        nc.sync.dma_start(w1_raw[:], w1.rearrange("(p j) c -> p j c", j=PACK))
        x_codes = sb("x_codes", [P, T], I32)
        nc.sync.dma_start(x_codes[:], x_words[0].rearrange("p n t -> p (n t)").bitcast(I32))
        nc.sync.dma_start(lists["n2"][:], n2)
        nc.sync.dma_start(lists["n1"][:], n1)
        gain = sb("gain", [P, PACK], F32)
        nc.sync.dma_start(gain[:], gn.rearrange("(p t) o -> p (t o)", t=PACK))
        w2_raw = sb("w2_raw", [P, PACK, N], F32)
        nc.sync.dma_start(w2_raw[:], w2.rearrange("(p j) c -> p j c", j=PACK))
        nc.sync.dma_start(lists["n4"][:], n4)
        nc.sync.dma_start(lists["n3"][:], n3)

        preload_in = sb("preload_in", [P, 8], F32)
        preload_out = sb("preload_out", [P, 8], F32)
        nc.vector.memset(preload_in[:], 1.0)
        nc.scalar.activation(preload_out[:], preload_in[:], ACT.Ln)
        ident = sb("ident", [P, P], F32)
        make_identity(nc, ident[:])

        picked_bytes = sb("picked_bytes", [P, S], U8)
        picked_codes = sb("picked_codes", [P, S], I32)
        nc.vector.tensor_copy(picked_bytes[:], x_bytes[:].indirect(lists["offs"][:]))

        w1_cols = w1_raw[:].rearrange("p j (m t) -> p t m j", t=PACK)
        w1_bf = [sb("w1_bf%d" % u, [P, 2, P, PACK], BF16, after=("x_bytes", None)[u]) for u in range(2)]
        nc.vector.tensor_copy(w1_bf[0][:], w1_cols[:, 0:2])
        nc.scalar.copy(w1_bf[1][:], w1_cols[:, 2:4])

        def quantise(name, source, width, after=None):
            codes = sb(name + "_codes", [P, width], U32, after=after)
            scales = sb(name + "_scales", [P, width], U8)
            nc.vector.quantize_mx(out=codes[:].bitcast(FP8X4), scales=scales[:], in_=source)
            return codes, scales

        def product(bank, stationary, block, moving_codes, moving_scales):
            codes, scales = stationary
            nc.tensor.matmul_mx(
                out=bank,
                lhsT=codes[:, block * P : (block + 1) * P].bitcast(FP8X4),
                lhsT_scale=scales[:, block * P : (block + 1) * P],
                rhs=moving_codes.bitcast(FP8X4),
                rhs_scale=moving_scales,
                start=True,
                stop=True,
            )

        w1_mx = [quantise("w1_lo", w1_bf[0][:].rearrange("p t m j -> p (t m j)"), 2 * P)]
        for lo in (0, HALF):
            nc.vector.tensor_copy(
                picked_codes[:, lo : lo + HALF].bitcast(U32),
                x_codes[:].bitcast(U32).indirect(entries("offs", lo, lo + HALF)),
            )
        w1_mx.append(quantise("w1_hi", w1_bf[1][:].rearrange("p t m j -> p (t m j)"), 2 * P, after="x_codes"))

        y_first_half = psum.tile([P, S], F32, name="y_first_half", tag="h_ps%d" % LAST)
        y_ps = [psum.tile([P, S], F32, name="y_ps%d" % t) for t in range(PACK)]
        y_parts = {0: [(0, HALF, y_first_half[:, :HALF]), (HALF, S, y_ps[0][:, :HALF])]}
        for t in range(1, PACK):
            y_parts[t] = [(0, S, y_ps[t][:])]
        for t in range(PACK):
            for lo, hi, bank in y_parts[t]:
                product(bank, w1_mx[t // 2], t % 2, picked_codes[:, lo:hi], picked_bytes[:, lo:hi])

        looked_up = [sb("looked_up%d" % t, [P, WINDOW], F32) for t in range(PACK)]
        size = [sb("size%d" % t, [P, WINDOW], F32) for t in range(PACK)]
        size_copy = {t: sb("size_copy%d" % t, [P, S], F32) for t in VECTOR_PLANES}

        def gained_y(t):
            for lo, hi, bank in y_parts[t]:
                nc.scalar.activation(looked_up[t][:, lo:hi], bank, ACT.Copy, scale=gain[:, t : t + 1])

        def size_of_y(t):
            for lo, hi, bank in y_parts[t]:
                nc.scalar.activation(size[t][:, lo:hi], bank, ACT.Abs)

        gained_y(0)
        gained_y(1)
        gained_y(2)
        size_of_y(0)
        gained_y(3)
        size_of_y(1)
        log_size = {t: sb("log_size%d" % t, [P, WINDOW], F32) for t in SCALAR_PLANES}
        far_size = {t: sb("far_size%d" % t, [P, S], F32) for t in SCALAR_PLANES}
        for t in SCALAR_PLANES:
            nc.scalar.activation(log_size[t][:, :S], size[t][:, :S], ACT.Ln, bias=0.25)
        for t in SCALAR_PLANES:
            nc.scalar.activation(far_size[t][:], log_size[t][:].indirect(lists["n4"][:]), ACT.Exp)
        for t in VECTOR_PLANES:
            size_of_y(t)
            nc.sync.dma_start(size_copy[t][:], size[t][:, :S])
        w2_bf = sb("w2_bf", [P, PACK, P, PACK], BF16)
        nc.scalar.copy(
            w2_bf[:].rearrange("p t m j -> p m j t"), w2_raw[:].rearrange("p j (m t) -> p m j t", t=PACK)
        )

        z_planes = sb("z_planes", [P, PACK, S], BF16)
        at_n2, diff, den, root, recip = {}, {}, {}, {}, {}

        def fetch_n2(t):
            at_n2[t] = sb("at_n2_%d" % t, [P, S], F32)
            nc.vector.tensor_copy(at_n2[t][:], looked_up[t][:].indirect(lists["n2"][:]))

        def difference(t, lo, hi, after=None):
            diff[t, lo] = sb("diff%d_%d" % (t, lo), [P, hi - lo], F32, after=after)
            nc.vector.tensor_tensor(
                diff[t, lo][:], looked_up[t][:].indirect(entries("n1", lo, hi)), at_n2[t][:, lo:hi], ALU.subtract
            )

        def z_plane(t, lo, hi):
            for a, b, bank in y_parts[t]:
                first, end = max(a, lo), min(b, hi)
                nc.vector.tensor_tensor(
                    z_planes[:, t, first:end],
                    diff[t, lo][:, first - lo : end - lo],
                    bank[:, first - a : end - a],
                    ALU.mult,
                )

        fetch_n2(0)
        fetch_n2(1)
        difference(0, 0, S)
        fetch_n2(2)
        z_plane(0, 0, S)
        difference(1, 0, S)
        fetch_n2(3)
        z_plane(1, 0, S)
        difference(2, 0, S)
        difference(LAST, 0, HALF, after="last_plane")
        z_plane(2, 0, S)
        z_plane(LAST, 0, HALF)
        difference(LAST, HALF, S, after="last_plane")

        for t in SCALAR_PLANES:
            den[t] = psum.tile([P, S], F32, name="den_turned%d" % t, tag="y_ps%d" % t)
            for c in range(S // P):
                cols = slice(c * P, (c + 1) * P)
                nc.tensor.matmul(den[t][:, cols], size[t][:, cols], ident[:], start=True, stop=False, is_transpose=True)
                nc.tensor.matmul(den[t][:, cols], far_size[t][:, cols], ident[:], start=False, stop=True, is_transpose=True)

        w2_mx = quantise("w2", w2_bf[:].rearrange("p t m j -> p (t m j)"), N, after="at_n2_%d" % LAST)
        z_plane(LAST, HALF, S)

        h_ps = [psum.tile([P, S], F32, name="h_ps%d" % t) for t in range(PACK)]

        def second_product(u, after):
            cols = slice(u * HALF, (u + 1) * HALF)
            z_words = sb("z_words%d" % u, [P, HALF, PACK], BF16)
            nc.scalar.copy(
                z_words[:].rearrange("p (c i) t -> p c t i", i=4),
                z_planes[:, :, cols].rearrange("p t (c i) -> p c t i", i=4),
            )
            codes, scales = quantise("z%d" % u, z_words[:].rearrange("p j t -> p (j t)"), HALF, after=after)
            for t in range(PACK):
                product(h_ps[t][:, cols], w2_mx, t, codes[:], scales[:])

        def denominator(t, after):
            den[t] = sb("den%d" % t, [P, S], F32, after=after)
            nc.vector.tensor_tensor(den[t][:], size[t][:].indirect(lists["n4"][:]), size_copy[t][:], ALU.add)

        second_product(0, after="last_plane")
        denominator(2, after="z_words0")
        second_product(1, after="size_copy2")
        denominator(3, after="z_words1")

        minus_h = {}

        def leave_psum(t):
            nc.scalar.activation(looked_up[t][:, :S], h_ps[t][:], ACT.Copy, scale=-1.0)

        def second_copy(t, lo, hi):
            minus_h[t, lo] = sb("minus_h%d_%d" % (t, lo), [P, hi - lo], F32)
            nc.scalar.activation(minus_h[t, lo][:], h_ps[t][:, lo:hi], ACT.Copy, scale=-1.0)

        def turned_root(t, lo, hi):
            nc.scalar.activation(root[t][:, lo:hi], den[t][:, lo:hi], ACT.Abs_reciprocal_sqrt, bias=0.25)

        def turned_reciprocal(t):
            back = psum.tile([P, S], F32, name="root_back%d" % t, tag="y_ps%d" % t)
            for c in range(S // P):
                cols = slice(c * P, (c + 1) * P)
                nc.tensor.transpose(back[:, cols], root[t][:, cols], ident[:])
            recip[t] = sb("recip%d" % t, [P, S], F32)
            nc.scalar.activation(recip[t][:], back[:], ACT.Square)

        def plain_reciprocal(t):
            root[t] = sb("root%d" % t, [P, S], F32)
            recip[t] = sb("recip%d" % t, [P, S], F32)
            nc.scalar.activation(root[t][:], den[t][:], ACT.Abs_reciprocal_sqrt, bias=0.5)
            nc.scalar.activation(recip[t][:], root[t][:], ACT.Square)

        root[0] = sb("root0", [P, S], F32, after="z_planes")
        turned_root(0, 0, P)
        for t in (0, 1):
            leave_psum(t)
            second_copy(t, 0, S)
        turned_root(0, P, S)
        leave_psum(2)
        second_copy(2, 0, S)
        turned_reciprocal(0)
        root[1] = sb("root1", [P, S], F32)
        turned_root(1, 0, S)
        leave_psum(LAST)
        turned_reciprocal(1)
        second_copy(LAST, 0, HALF)
        second_copy(LAST, HALF, S)
        for t in VECTOR_PLANES:
            plain_reciprocal(t)

        out_rows = out.rearrange("(p t) j -> p t j", t=PACK)
        numer = {}

        def numerator(t, lo, hi, after=None):
            numer[t, lo] = sb("numer%d_%d" % (t, lo), [P, hi - lo], F32, after=after)
            nc.vector.tensor_tensor(
                numer[t, lo][:], looked_up[t][:].indirect(entries("n3", lo, hi)), minus_h[t, lo][:], ALU.subtract
            )

        def finish(t, lo, hi, after=None):
            result = sb("result%d_%d" % (t, lo), [P, hi - lo], F32, after=after)
            nc.vector.tensor_tensor(result[:], numer[t, lo][:], recip[t][:, lo:hi], ALU.mult)
            nc.sync.dma_start(out_rows[:, t, lo:hi], result[:])

        numerator(0, 0, S, after="size_copy3")
        numerator(1, 0, S)
        numerator(2, 0, S)
        finish(0, 0, S, after="minus_h2_0")
        numerator(LAST, 0, HALF)
        finish(1, 0, S, after="minus_h%d_0" % LAST)
        numerator(LAST, HALF, S)
        finish(2, 0, S, after="minus_h%d_%d" % (LAST, HALF))
        finish(LAST, 0, HALF)
        finish(LAST, HALF, S)
